import numpy as np, ml_dtypes
CORES = [17,81,89,18,82,90]
N = 6
import mx_ref
NC, WT = 128, 2
LR = np.float32(2.0 ** -2)
BF = ml_dtypes.bfloat16
def cut(t, i, w=512):
    return t[:, w * i:w * i + w]
def tile(rs):
    return np.stack(rs, axis=2).reshape(128, -1).astype(BF)
def pick(b):
    s = np.zeros((128, 128, 4), np.float32)
    s[np.arange(128), np.arange(128), b] = 1.0
    return mx_ref.quantize(s.reshape(128, 512).astype(BF))
def pk(c, s, i=0):
    return (np.ascontiguousarray(c[:, 512 * i:512 * i + 512]), mx_ref.live(s[:, 128 * i:128 * i + 128]))
def inputs(rng, e, E):
    def f(*shape):
        v = (rng.standard_normal(shape, dtype=np.float32) * np.exp2(rng.integers(-2, 3, shape[:-1] + (1,)))).astype(BF)
        return mx_ref.spread((v.astype(np.float32) * np.exp2(rng.integers(-E, E + 1, shape[:-2] + (1, 1))).astype(np.float32)).astype(BF), rng, e)
    def packed(k):
        c = np.zeros((N, 128, k * 512), np.uint8); s = np.zeros((N, 128, k * 128), np.uint8)
        for r in range(N):
            for i in range(k):
                a, b = mx_ref.quantize(f(128, 512)); c[r][:, 512 * i:512 * i + 512] = a; s[r][:, 128 * i:128 * i + 128] = mx_ref.plane(b, rng)
        return c, s
    d = {}
    d["wc"], d["ws"] = packed(WT)
    d["gr"] = f(N, 128, WT * 512)
    d["x"] = f(N, 128, 4 * NC)
    return d
def setup_inputs(rng):
    return inputs(rng, 0, 0)
def setup_inputs_blocks(rng):
    return inputs(rng, 2, 0)
def setup_inputs_wide(rng):
    return inputs(rng, 0, 4)
def setup_inputs_faint(rng):
    d = setup_inputs(rng); d["gr"] = mx_ref.flush((d["gr"].astype(np.float32) * np.float32(2.0 ** -12)).astype(BF))
    return d
def reference(wc, ws, gr, x):
    S = [pick(t) for t in range(4)]
    H = [mx_ref.quantize(tile([mx_ref.matmul(S[t], pk(wc[j], ws[j], i)) - cut(gr[j], i).astype(np.float32)[:, t::4] * LR for t in range(4)])) for j in range(N) for i in range(WT)]
    y = np.zeros((N, 128, N * WT * NC), np.float32)
    for r in range(N):
        X = mx_ref.quantize(x[r])
        for b in range(N * WT):
            y[r][:, NC * b:NC * b + NC] = mx_ref.matmul(H[b], X)
    return {"y": y}

@@ -1,0 +1,214 @@
+from concourse.bass import DstId, RemoteDMATransfer
+from concourse.mybir import dt, AluOpType, ActivationFunctionType
+
+N, WT, NC = 6, 2, 128
+TC = 4 * NC
+GW = WT * NC
+SIM_CORES = 96
+
+SCRATCH = {
+    "z": ("sbuf", [128, TC + 4], "bfloat16"),
+    "sq": ("sbuf", [128, 4 * NC], "float8_e4m3fn_x4"),
+    "ss": ("sbuf", [128, 4 * NC], "uint8"),
+    "wq": ("sbuf", [128, GW], "float8_e4m3fn_x4"),
+    "wp": ("sbuf", [128, GW], "uint8"),
+    "gb": ("sbuf", [128, WT * TC], "bfloat16"),
+    "gs": ("sbuf", [128, WT * TC], "bfloat16"),
+    "v": ("sbuf", [128, WT * TC], "bfloat16"),
+    "xb": ("sbuf", [128, TC], "bfloat16"),
+    "xq": ("sbuf", [128, NC], "float8_e4m3fn_x4"),
+    "xp": ("sbuf", [128, NC], "uint8"),
+    "qc": ("sbuf", [128, N * GW], "float8_e4m3fn_x4"),
+    "qs": ("sbuf", [128, N * GW], "uint8"),
+    "yb": ("sbuf", [128, N * GW], "float32"),
+    "ps": ("psum", [128, 4096], "float32"),
+}
+PIECES = ("c0", "c1", "p")
+SEMAPHORES = (["zf", "zd", "sqd", "lw0", "lw1", "lp", "lg0", "lg1", "lx", "pg0", "pg1", "md", "vd", "qd", "xd",
+               "mv", "ms", "cv", "cs", "ys", "sent"]
+              + ["a%d%s" % (j, p) for j in range(N) for p in PIECES])
+
+
+def bits(m):
+    return bin(m).count("1")
+
+
+def plan(cores, topo):
+    chips = []
+    for c in cores:
+        if topo.chip(c) not in chips:
+            chips.append(topo.chip(c))
+    members = {k: [c for c in cores if topo.chip(c) == k] for k in chips}
+    spare = {k: [c for c in range(SIM_CORES) if topo.chip(c) == k and c not in cores] for k in chips}
+    load = {}
+    first = {c: [] for c in cores}
+    relays = []
+    far = [(s, k) for s in cores for k in sorted(chips) if k != topo.chip(s)]
+    direct = [(s, k) for s, k in far if topo.may_write(s, members[k][0])]
+    for s, k in direct:
+        w = (topo.chip(s), topo.die(s))
+        load[w] = load.get(w, 0) + 1
+    for s, k in far:
+        if (s, k) in direct:
+            continue
+        own = [h for h in spare[topo.chip(s)] if topo.may_write(h, members[k][0])]
+        h = min(own, key=lambda h: (load.get((topo.chip(h), topo.die(h)), 0), topo.die(h) != topo.die(s), h))
+        spare[topo.chip(s)].remove(h)
+        w = (topo.chip(h), topo.die(h))
+        load[w] = load.get(w, 0) + len(members[k])
+        first[s].append(h)
+        relays.append((h, s, members[k]))
+    for s, k in direct:
+        h = min(spare[k], key=lambda h: (topo.die(h) != topo.die(members[k][0]), h))
+        spare[k].remove(h)
+        first[s].append(h)
+        relays.append((h, s, members[k]))
+    sends = {}
+
+    def add(c, src, dests):
+        off = [d for d in dests if topo.chip(d) != topo.chip(c)]
+        on = [d for d in dests if topo.chip(d) == topo.chip(c)]
+        tr, om = [], 0
+        if off:
+            om = topo.mask(c, off[0])
+            tr.append((om, off))
+        if on:
+            tr.append((topo.mask(c, on[0]) & ~om, on))
+        sends.setdefault(c, []).append((cores.index(src), tr))
+
+    for s in cores:
+        add(s, s, first[s] + [c for c in members[topo.chip(s)] if c != s])
+    for h, s, ds in relays:
+        add(h, s, ds)
+    got = {}
+    for c in sends:
+        for j, tr in sends[c]:
+            for m, ds in tr:
+                for d in ds:
+                    got[(d, j)] = bits(m)
+    return sends, got
+
+
+def piece(T, j, p):
+    a = GW * j
+    if p == "p":
+        return T.qs[:, a:a + GW]
+    i = int(p[1])
+    return T.qc[:, a + NC * i:a + NC * (i + 1)].bitcast(dt.uint8)
+
+
+def send(g, T, topo, j, p, tr):
+    ap = piece(T, j, p)
+    ts = []
+    for m, ds in tr:
+        ids = []
+        for d in ds:
+            a = topo.addr(d)
+            ids.append(DstId(rid=a[0], pnc=a[1]))
+        ts.append(RemoteDMATransfer(dst_ids=ids, dma_engine_mask=m, remote_sem=T.sem["a%d%s" % (j, p)],
+                                    srcs=[ap], dsts=[ap] * len(ds)))
+    g.remote_dma_fused(ts, local_sem=T.sem.sent)
+    return sum(bits(m) for m, ds in tr)
+
+
+def rank_program(g, core, T, topo):
+    cores = list(T.cores)
+    sends, got = plan(cores, topo)
+    rank = T.rank_of(core)
+    if rank is None:
+        n = 0
+        for p in PIECES:
+            for j, tr in sends.get(core, []):
+                g.wait_ge(T.sem["a%d%s" % (j, p)], got[(core, j)])
+                n += send(g, T, topo, j, p, tr)
+        if n:
+            g.wait_ge(T.sem.sent, n)
+        return
+
+    sem = T.sem
+    me = GW * rank
+    sy, sc, ve, te = g.sync, g.scalar, g.vector, g.tensor
+
+    sy.dma_start(T.gb[:, 0:TC], T.gr[:, 0:TC]).then_inc(sem.lg0, 16)
+    sc.dma_start(T.wq[:, 0:NC].bitcast(dt.uint8), T.wc[:, 0:TC]).then_inc(sem.lw0, 16)
+    sc.dma_start(T.wp[:, :], T.ws[:, :]).then_inc(sem.lp, 16)
+    sy.dma_start(T.wq[:, NC:GW].bitcast(dt.uint8), T.wc[:, TC:2 * TC]).then_inc(sem.lw1, 16)
+    sc.dma_start(T.gb[:, TC:2 * TC], T.gr[:, TC:2 * TC]).then_inc(sem.lg1, 16)
+    sy.dma_start(T.xb[:, :], T.x[:, :]).then_inc(sem.lx, 16)
+
+    ve.memset(T.z[:, :], 0.0).then_inc(sem.zf, 1)
+    g.wait_ge(sem.zf, 1)
+    g.affine_select(T.z[:, :], T.z[:, :], [[-1, TC + 4]], AluOpType.not_equal, 1.0, 3, 4).then_inc(sem.zd, 1)
+    ve.wait_ge(sem.zd, 1)
+    for b in range(4):
+        ve.quantize_mx(T.sq[:, NC * b:NC * b + NC], T.ss[:, NC * b:NC * b + NC],
+                       T.z[:, 3 - b:3 - b + TC]).then_inc(sem.sqd, 1)
+
+    te.wait_ge(sem.sqd, 4)
+    te.wait_ge(sem.lp, 16)
+    for i in range(WT):
+        te.wait_ge(sem["lw%d" % i], 16)
+        for b in range(4):
+            o = 512 * (4 * i + b)
+            te.matmul_mx(T.ps[:, o:o + NC], T.sq[:, NC * b:NC * b + NC], T.ss[:, NC * b:NC * b + NC],
+                         T.wq[:, NC * i:NC * i + NC], T.wp[:, NC * i:NC * i + NC], True, True).then_inc(sem.md, 1)
+
+    ve.wait_ge(sem.lg0, 16)
+    ve.tensor_scalar(T.gs[:, 0:TC], T.gb[:, 0:TC], 0.25, None, AluOpType.mult).then_inc(sem.pg0, 1)
+    sc.wait_ge(sem.lg1, 16)
+    sc.activation(T.gs[:, TC:2 * TC], T.gb[:, TC:2 * TC], ActivationFunctionType.Copy, scale=0.25).then_inc(sem.pg1, 1)
+
+    for i in range(WT):
+        ve.wait_ge(sem["pg%d" % i], 1)
+        for b in range(4):
+            k = 4 * i + b
+            ve.wait_ge(sem.md, k + 1)
+            c0, c1 = TC * i + b, TC * (i + 1)
+            ve.tensor_tensor(T.v[:, c0:c1:4], T.ps[:, 512 * k:512 * k + NC], T.gs[:, c0:c1:4],
+                             AluOpType.subtract).then_inc(sem.vd, 1)
+        ve.wait_ge(sem.vd, 4 * (i + 1))
+        ve.quantize_mx(T.qc[:, me + NC * i:me + NC * i + NC], T.qs[:, me + NC * i:me + NC * i + NC],
+                       T.v[:, TC * i:TC * (i + 1)]).then_inc(sem.qd, 1)
+    ve.wait_ge(sem.lx, 16)
+    ve.quantize_mx(T.xq[:, :], T.xp[:, :], T.xb[:, :]).then_inc(sem.xd, 1)
+
+    n = 0
+    for p, need in (("c0", 1), ("c1", 2), ("p", 2)):
+        g.wait_ge(sem.qd, need)
+        for j, tr in sends[core]:
+            n += send(g, T, topo, j, p, tr)
+
+    def dist(j):
+        a, b = topo.chip(core), topo.chip(cores[j])
+        if j == rank:
+            return 0
+        return 1 if a == b else 2 if topo.same_plane(a, b) else 3 if topo.mates(a, b) else 4
+
+    order = sorted(range(N), key=lambda j: (dist(j), j))
+    te.wait_ge(sem.qd, 2)
+    te.wait_ge(sem.xd, 1)
+    for k, j in enumerate(order):
+        if k >= 4:
+            te.wait_ge(sem.cv, k - 3)
+            te.wait_ge(sem.cs, k - 3)
+        for i in range(WT):
+            if j != rank:
+                te.wait_ge(sem["a%dc%d" % (j, i)], got[(core, j)])
+                if i == 0:
+                    te.wait_ge(sem["a%dp" % j], got[(core, j)])
+            o = 512 * (2 * (k % 4) + i)
+            a = GW * j + NC * i
+            te.matmul_mx(T.ps[:, o:o + NC], T.qc[:, a:a + NC], T.qs[:, a:a + NC], T.xq[:, :], T.xp[:, :],
+                         True, True).then_inc(sem.ms if i else sem.mv, 1)
+            if i == 0:
+                ve.wait_ge(sem.mv, k + 1)
+                ve.tensor_copy(T.yb[:, a:a + NC], T.ps[:, o:o + NC]).then_inc(sem.cv, 1)
+            else:
+                sc.wait_ge(sem.ms, k + 1)
+                sc.activation(T.yb[:, a:a + NC], T.ps[:, o:o + NC], ActivationFunctionType.Copy).then_inc(sem.cs, 1)
+        sy.wait_ge(sem.cv, k + 1)
+        sy.wait_ge(sem.cs, k + 1)
+        sy.dma_start(T.y[:, GW * j:GW * j + GW], T.yb[:, GW * j:GW * j + GW]).then_inc(sem.ys, 16)
+
+    g.wait_ge(sem.sent, n)
+    sy.wait_ge(sem.ys, 16 * N)

@@ -23,10 +23,10 @@ SCRATCH = {
     "yb": ("sbuf", [128, N * GW], "float32"),
     "ps": ("psum", [128, 4096], "float32"),
 }
-PIECES = ("c0", "c1", "p")
+PIECES = (("c0", 1), ("p", 2), ("c1", 2))
 SEMAPHORES = (["zf", "zd", "sqd", "lw0", "lw1", "lp", "lg0", "lg1", "lx", "pg0", "pg1", "md", "vd", "qd", "xd",
                "mv", "ms", "cv", "cs", "ys", "sent"]
-              + ["a%d%s" % (j, p) for j in range(N) for p in PIECES])
+              + ["a%d%s" % (j, p) for j in range(N) for p, need in PIECES])
 
 
 def bits(m):
@@ -117,7 +117,7 @@ def rank_program(g, core, T, topo):
     rank = T.rank_of(core)
     if rank is None:
         n = 0
-        for p in PIECES:
+        for p, need in PIECES:
             for j, tr in sends.get(core, []):
                 g.wait_ge(T.sem["a%d%s" % (j, p)], got[(core, j)])
                 n += send(g, T, topo, j, p, tr)
@@ -129,16 +129,15 @@ def rank_program(g, core, T, topo):
     me = GW * rank
     sy, sc, ve, te = g.sync, g.scalar, g.vector, g.tensor
 
-    sy.dma_start(T.gb[:, 0:TC], T.gr[:, 0:TC]).then_inc(sem.lg0, 16)
-    sc.dma_start(T.wq[:, 0:NC].bitcast(dt.uint8), T.wc[:, 0:TC]).then_inc(sem.lw0, 16)
     sc.dma_start(T.wp[:, :], T.ws[:, :]).then_inc(sem.lp, 16)
-    sy.dma_start(T.wq[:, NC:GW].bitcast(dt.uint8), T.wc[:, TC:2 * TC]).then_inc(sem.lw1, 16)
-    sc.dma_start(T.gb[:, TC:2 * TC], T.gr[:, TC:2 * TC]).then_inc(sem.lg1, 16)
+    for i in range(WT):
+        sy.dma_start(T.wq[:, NC * i:NC * i + NC].bitcast(dt.uint8), T.wc[:, TC * i:TC * i + TC]).then_inc(sem["lw%d" % i], 16)
+        sy.dma_start(T.gb[:, TC * i:TC * i + TC], T.gr[:, TC * i:TC * i + TC]).then_inc(sem["lg%d" % i], 16)
     sy.dma_start(T.xb[:, :], T.x[:, :]).then_inc(sem.lx, 16)
 
     ve.memset(T.z[:, :], 0.0).then_inc(sem.zf, 1)
     g.wait_ge(sem.zf, 1)
-    g.affine_select(T.z[:, :], T.z[:, :], [[-1, TC + 4]], AluOpType.not_equal, 1.0, 3, 4).then_inc(sem.zd, 1)
+    g.affine_select(T.z[:, 3:TC:4], T.z[:, 3:TC:4], [[-1, NC]], AluOpType.not_equal, 1.0, 0, 1).then_inc(sem.zd, 1)
     ve.wait_ge(sem.zd, 1)
     for b in range(4):
         ve.quantize_mx(T.sq[:, NC * b:NC * b + NC], T.ss[:, NC * b:NC * b + NC],
@@ -173,10 +172,11 @@ def rank_program(g, core, T, topo):
     ve.quantize_mx(T.xq[:, :], T.xp[:, :], T.xb[:, :]).then_inc(sem.xd, 1)
 
     n = 0
-    for p, need in (("c0", 1), ("c1", 2), ("p", 2)):
+    for p, need in PIECES:
         g.wait_ge(sem.qd, need)
         for j, tr in sends[core]:
             n += send(g, T, topo, j, p, tr)
+    sy.wait_ge(sem.sent, n)
 
     def dist(j):
         a, b = topo.chip(core), topo.chip(cores[j])
@@ -184,31 +184,34 @@ def rank_program(g, core, T, topo):
             return 0
         return 1 if a == b else 2 if topo.same_plane(a, b) else 3 if topo.mates(a, b) else 4
 
-    order = sorted(range(N), key=lambda j: (dist(j), j))
+    ranks = sorted(range(N), key=lambda j: (dist(j), j))
+    near = [j for j in ranks if dist(j) < 2]
+    blocks = [(j, i) for j in near for i in range(WT)] + [(j, i) for i in range(WT) for j in ranks if j not in near]
     te.wait_ge(sem.qd, 2)
     te.wait_ge(sem.xd, 1)
-    for k, j in enumerate(order):
-        if k >= 4:
-            te.wait_ge(sem.cv, k - 3)
-            te.wait_ge(sem.cs, k - 3)
-        for i in range(WT):
-            if j != rank:
-                te.wait_ge(sem["a%dc%d" % (j, i)], got[(core, j)])
-                if i == 0:
-                    te.wait_ge(sem["a%dp" % j], got[(core, j)])
-            o = 512 * (2 * (k % 4) + i)
-            a = GW * j + NC * i
-            te.matmul_mx(T.ps[:, o:o + NC], T.qc[:, a:a + NC], T.qs[:, a:a + NC], T.xq[:, :], T.xp[:, :],
-                         True, True).then_inc(sem.ms if i else sem.mv, 1)
+    for k, (j, i) in enumerate(blocks):
+        mm, cp = (sem.ms, sem.cs) if k % 2 else (sem.mv, sem.cv)
+        if k >= 8:
+            te.wait_ge(cp, (k - 8) // 2 + 1)
+        if j != rank:
+            te.wait_ge(sem["a%dc%d" % (j, i)], got[(core, j)])
             if i == 0:
-                ve.wait_ge(sem.mv, k + 1)
-                ve.tensor_copy(T.yb[:, a:a + NC], T.ps[:, o:o + NC]).then_inc(sem.cv, 1)
-            else:
-                sc.wait_ge(sem.ms, k + 1)
-                sc.activation(T.yb[:, a:a + NC], T.ps[:, o:o + NC], ActivationFunctionType.Copy).then_inc(sem.cs, 1)
-        sy.wait_ge(sem.cv, k + 1)
-        sy.wait_ge(sem.cs, k + 1)
-        sy.dma_start(T.y[:, GW * j:GW * j + GW], T.yb[:, GW * j:GW * j + GW]).then_inc(sem.ys, 16)
+                te.wait_ge(sem["a%dp" % j], got[(core, j)])
+        o = 512 * (k % 8)
+        a = GW * j + NC * i
+        te.matmul_mx(T.ps[:, o:o + NC], T.qc[:, a:a + NC], T.qs[:, a:a + NC], T.xq[:, :], T.xp[:, :],
+                     True, True).then_inc(mm, 1)
+        if k % 2:
+            sc.wait_ge(mm, k // 2 + 1)
+            sc.activation(T.yb[:, a:a + NC], T.ps[:, o:o + NC], ActivationFunctionType.Copy).then_inc(cp, 1)
+        else:
+            ve.wait_ge(mm, k // 2 + 1)
+            ve.tensor_copy(T.yb[:, a:a + NC], T.ps[:, o:o + NC]).then_inc(cp, 1)
+        sy.wait_ge(cp, k // 2 + 1)
+        if j not in near:
+            sy.dma_start(T.y[:, a:a + NC], T.yb[:, a:a + NC]).then_inc(sem.ys, 16)
+        elif i == WT - 1:
+            sy.dma_start(T.y[:, GW * j:GW * j + GW], T.yb[:, GW * j:GW * j + GW]).then_inc(sem.ys, 16)
 
     g.wait_ge(sem.sent, n)
-    sy.wait_ge(sem.ys, 16 * N)
+    sy.wait_ge(sem.ys, 16 * (len(near) + WT * (N - len(near))))

@@ -5,15 +5,16 @@ N, WT, NC = 6, 2, 128
 TC = 4 * NC
 GW = WT * NC
 SIM_CORES = 96
+UP = 4.0
 
 SCRATCH = {
     "z": ("sbuf", [128, TC + 4], "bfloat16"),
+    "cmp": ("sbuf", [128, NC], "bfloat16"),
     "sq": ("sbuf", [128, 4 * NC], "float8_e4m3fn_x4"),
     "ss": ("sbuf", [128, 4 * NC], "uint8"),
     "wq": ("sbuf", [128, GW], "float8_e4m3fn_x4"),
     "wp": ("sbuf", [128, GW], "uint8"),
     "gb": ("sbuf", [128, WT * TC], "bfloat16"),
-    "gs": ("sbuf", [128, WT * TC], "bfloat16"),
     "v": ("sbuf", [128, WT * TC], "bfloat16"),
     "xb": ("sbuf", [128, TC], "bfloat16"),
     "xq": ("sbuf", [128, NC], "float8_e4m3fn_x4"),
@@ -23,14 +24,22 @@ SCRATCH = {
     "yb": ("sbuf", [128, N * GW], "float32"),
     "ps": ("psum", [128, 4096], "float32"),
 }
-PIECES = (("c0", 1), ("p", 2), ("c1", 2))
-SEMAPHORES = (["zf", "zd", "sqd", "lw0", "lw1", "lp", "lg0", "lg1", "lx", "pg0", "pg1", "md", "vd", "qd", "xd",
-               "mv", "ms", "cv", "cs", "ys", "sent"]
-              + ["a%d%s" % (j, p) for j in range(N) for p, need in PIECES])
+FAR = ("c0", "p", "c1")
+NEAR = ("c", "p")
+TILES = {"c0": 1, "p": 2, "c1": 2, "c": 2}
+ORDER = (("own", 0), ("own", 1), ("near", 0), ("near", 1), ("direct", 0), ("direct", 1), ("later", 0), ("later", 1),
+         ("passed", 0), ("helper", 0), ("relay", 0), ("passed", 1), ("helper", 1), ("relay", 1))
+SEMAPHORES = (["cd", "zd", "sqd", "lw0", "lw1", "lp", "lg0", "lg1", "lx", "md", "vd", "qd", "xd",
+               "mv", "ms", "cv", "cs", "ys", "sent", "nsent"]
+              + ["a%d%s" % (j, p) for j in range(N) for p in TILES])
 
 
 def bits(m):
     return bin(m).count("1")
+
+
+def hops(topo, a, b):
+    return 0 if a == b else 1 if topo.same_plane(a, b) else 2 if topo.mates(a, b) else 3
 
 
 def plan(cores, topo):
@@ -41,8 +50,11 @@ def plan(cores, topo):
     members = {k: [c for c in cores if topo.chip(c) == k] for k in chips}
     spare = {k: [c for c in range(SIM_CORES) if topo.chip(c) == k and c not in cores] for k in chips}
     load = {}
-    first = {c: [] for c in cores}
-    relays = []
+    on = {c: [] for c in cores}
+    off = {c: [] for c in cores}
+    ways = {}
+    passed = {}
+    way = {(c, cores.index(c)): "own" for c in cores}
     far = [(s, k) for s in cores for k in sorted(chips) if k != topo.chip(s)]
     direct = [(s, k) for s, k in far if topo.may_write(s, members[k][0])]
     for s, k in direct:
@@ -56,48 +68,82 @@ def plan(cores, topo):
         spare[topo.chip(s)].remove(h)
         w = (topo.chip(h), topo.die(h))
         load[w] = load.get(w, 0) + len(members[k])
-        first[s].append(h)
-        relays.append((h, s, members[k]))
-    for s, k in direct:
-        h = min(spare[k], key=lambda h: (topo.die(h) != topo.die(members[k][0]), h))
-        spare[k].remove(h)
-        first[s].append(h)
-        relays.append((h, s, members[k]))
-    sends = {}
+        on[s].append(h)
+        ways[(h, s)] = {p: list(members[k]) for p in FAR}
+        for d in members[k]:
+            way[(d, cores.index(s))] = "helper"
+    for s in cores:
+        if not on[s]:
+            continue
+        own = [h for h in spare[topo.chip(s)] if all(topo.may_write(h, ways[(r, s)][FAR[0]][0]) for r in on[s])]
+        x = min(own, key=lambda x: (sum(topo.die(x) == topo.die(r) for r in on[s]), x))
+        spare[topo.chip(s)].remove(x)
+        ways[(x, s)] = {FAR[0]: []}
+        for r in on[s]:
+            ways[(x, s)][FAR[0]] += ways[(r, s)][FAR[0]][1:]
+            ways[(r, s)][FAR[0]] = ways[(r, s)][FAR[0]][:1]
+        on[s].append(x)
+    for s, k in sorted(direct, key=lambda w: hops(topo, topo.chip(w[0]), w[1])):
+        j = cores.index(s)
+        free = [h for h in members[k] if h not in [d for d, t in passed]]
+        if free:
+            h = free[0]
+            passed[(h, s)] = [d for d in members[k] if d != h]
+        else:
+            h = min(spare[k], key=lambda h: (topo.die(h) != topo.die(members[k][0]), h))
+            spare[k].remove(h)
+            ways[(h, s)] = {p: list(members[k]) for p in FAR}
+        off[s].append(h)
+        for d in members[k]:
+            way[(d, j)] = "direct" if d == h else "passed" if free else "relay"
+    for s in cores:
+        for d in members[topo.chip(s)]:
+            if d != s:
+                way[(d, cores.index(s))] = "later" if on[s] else "near"
+    calls, got = {}, {}
 
-    def add(c, src, dests):
-        off = [d for d in dests if topo.chip(d) != topo.chip(c)]
-        on = [d for d in dests if topo.chip(d) == topo.chip(c)]
-        tr, om = [], 0
-        if off:
-            om = topo.mask(c, off[0])
-            tr.append((om, off))
-        if on:
-            tr.append((topo.mask(c, on[0]) & ~om, on))
-        sends.setdefault(c, []).append((cores.index(src), tr))
+    def add(c, s, p, tr, local):
+        calls.setdefault(c, []).append((cores.index(s), p, tr, local))
+        for m, ds in tr:
+            for d in ds:
+                got[(d, cores.index(s), p)] = bits(m)
 
     for s in cores:
-        add(s, s, first[s] + [c for c in members[topo.chip(s)] if c != s])
-    for h, s, ds in relays:
-        add(h, s, ds)
-    got = {}
-    for c in sends:
-        for j, tr in sends[c]:
-            for m, ds in tr:
-                for d in ds:
-                    got[(d, j)] = bits(m)
-    return sends, got
+        nb = [c for c in members[topo.chip(s)] if c != s]
+        other = [c for c in cores if topo.chip(c) != topo.chip(s)]
+        om = topo.mask(s, other[0])
+        every = topo.mask(s, nb[0])
+        rest = every & ~om
+        for p in FAR:
+            tr = []
+            if off[s]:
+                tr.append((om, off[s]))
+            hs = [h for h in on[s] if p in ways[(h, s)]]
+            if hs:
+                tr.append((rest if off[s] else every, hs))
+            add(s, s, p, tr, "sent")
+        for p in NEAR:
+            add(s, s, p, [(every if not off[s] else om if on[s] else rest, nb)], "nsent")
+    for p in FAR:
+        for (h, s), ds in passed.items():
+            add(h, s, p, [(topo.mask(h, ds[0]), ds)], "nsent")
+        for (h, s), w in ways.items():
+            if p in w:
+                add(h, s, p, [(topo.mask(h, w[p][0]), w[p])], "sent")
+    return calls, got, way
 
 
 def piece(T, j, p):
     a = GW * j
     if p == "p":
         return T.qs[:, a:a + GW]
+    if p == "c":
+        return T.qc[:, a:a + GW].bitcast(dt.uint8)
     i = int(p[1])
     return T.qc[:, a + NC * i:a + NC * (i + 1)].bitcast(dt.uint8)
 
 
-def send(g, T, topo, j, p, tr):
+def send(g, T, topo, j, p, tr, local):
     ap = piece(T, j, p)
     ts = []
     for m, ds in tr:
@@ -107,20 +153,19 @@ def send(g, T, topo, j, p, tr):
             ids.append(DstId(rid=a[0], pnc=a[1]))
         ts.append(RemoteDMATransfer(dst_ids=ids, dma_engine_mask=m, remote_sem=T.sem["a%d%s" % (j, p)],
                                     srcs=[ap], dsts=[ap] * len(ds)))
-    g.remote_dma_fused(ts, local_sem=T.sem.sent)
+    g.remote_dma_fused(ts, local_sem=T.sem[local])
     return sum(bits(m) for m, ds in tr)
 
 
 def rank_program(g, core, T, topo):
     cores = list(T.cores)
-    sends, got = plan(cores, topo)
+    calls, got, way = plan(cores, topo)
     rank = T.rank_of(core)
     if rank is None:
         n = 0
-        for p, need in PIECES:
-            for j, tr in sends.get(core, []):
-                g.wait_ge(T.sem["a%d%s" % (j, p)], got[(core, j)])
-                n += send(g, T, topo, j, p, tr)
+        for j, p, tr, local in calls.get(core, []):
+            g.wait_ge(T.sem["a%d%s" % (j, p)], got[(core, j, p)])
+            n += send(g, T, topo, j, p, tr, local)
         if n:
             g.wait_ge(T.sem.sent, n)
         return
@@ -135,35 +180,33 @@ def rank_program(g, core, T, topo):
         sy.dma_start(T.gb[:, TC * i:TC * i + TC], T.gr[:, TC * i:TC * i + TC]).then_inc(sem["lg%d" % i], 16)
     sy.dma_start(T.xb[:, :], T.x[:, :]).then_inc(sem.lx, 16)
 
-    ve.memset(T.z[:, :], 0.0).then_inc(sem.zf, 1)
-    g.wait_ge(sem.zf, 1)
-    g.affine_select(T.z[:, 3:TC:4], T.z[:, 3:TC:4], [[-1, NC]], AluOpType.not_equal, 1.0, 0, 1).then_inc(sem.zd, 1)
+    g.iota(T.cmp[:, :], [[1, NC]], 0, -1, allow_small_or_imprecise_dtypes=True).then_inc(sem.cd, 1)
+    ve.memset(T.z[:, :], 0.0).then_inc(sem.zd, 1)
     ve.wait_ge(sem.zd, 1)
+    ve.wait_ge(sem.cd, 1)
+    ve.tensor_scalar(T.z[:, 3:TC:4], T.cmp[:, :], 0.0, UP, AluOpType.is_equal, AluOpType.mult).then_inc(sem.zd, 1)
+    ve.wait_ge(sem.zd, 2)
     for b in range(4):
         ve.quantize_mx(T.sq[:, NC * b:NC * b + NC], T.ss[:, NC * b:NC * b + NC],
                        T.z[:, 3 - b:3 - b + TC]).then_inc(sem.sqd, 1)
 
-    te.wait_ge(sem.sqd, 4)
     te.wait_ge(sem.lp, 16)
     for i in range(WT):
         te.wait_ge(sem["lw%d" % i], 16)
         for b in range(4):
+            if i == 0:
+                te.wait_ge(sem.sqd, b + 1)
             o = 512 * (4 * i + b)
             te.matmul_mx(T.ps[:, o:o + NC], T.sq[:, NC * b:NC * b + NC], T.ss[:, NC * b:NC * b + NC],
                          T.wq[:, NC * i:NC * i + NC], T.wp[:, NC * i:NC * i + NC], True, True).then_inc(sem.md, 1)
 
-    ve.wait_ge(sem.lg0, 16)
-    ve.tensor_scalar(T.gs[:, 0:TC], T.gb[:, 0:TC], 0.25, None, AluOpType.mult).then_inc(sem.pg0, 1)
-    sc.wait_ge(sem.lg1, 16)
-    sc.activation(T.gs[:, TC:2 * TC], T.gb[:, TC:2 * TC], ActivationFunctionType.Copy, scale=0.25).then_inc(sem.pg1, 1)
-
     for i in range(WT):
-        ve.wait_ge(sem["pg%d" % i], 1)
+        ve.wait_ge(sem["lg%d" % i], 16)
         for b in range(4):
             k = 4 * i + b
             ve.wait_ge(sem.md, k + 1)
             c0, c1 = TC * i + b, TC * (i + 1)
-            ve.tensor_tensor(T.v[:, c0:c1:4], T.ps[:, 512 * k:512 * k + NC], T.gs[:, c0:c1:4],
+            ve.tensor_tensor(T.v[:, c0:c1:4], T.ps[:, 512 * k:512 * k + NC], T.gb[:, c0:c1:4],
                              AluOpType.subtract).then_inc(sem.vd, 1)
         ve.wait_ge(sem.vd, 4 * (i + 1))
         ve.quantize_mx(T.qc[:, me + NC * i:me + NC * i + NC], T.qs[:, me + NC * i:me + NC * i + NC],
@@ -171,22 +214,18 @@ def rank_program(g, core, T, topo):
     ve.wait_ge(sem.lx, 16)
     ve.quantize_mx(T.xq[:, :], T.xp[:, :], T.xb[:, :]).then_inc(sem.xd, 1)
 
-    n = 0
-    for p, need in PIECES:
-        g.wait_ge(sem.qd, need)
-        for j, tr in sends[core]:
-            n += send(g, T, topo, j, p, tr)
-    sy.wait_ge(sem.sent, n)
-
-    def dist(j):
-        a, b = topo.chip(core), topo.chip(cores[j])
+    n = {"sent": 0, "nsent": 0}
+    for j, p, tr, local in calls[core]:
         if j == rank:
-            return 0
-        return 1 if a == b else 2 if topo.same_plane(a, b) else 3 if topo.mates(a, b) else 4
+            g.wait_ge(sem.qd, TILES[p])
+        else:
+            g.wait_ge(sem["a%d%s" % (j, p)], got[(core, j, p)])
+        n[local] += send(g, T, topo, j, p, tr, local)
+    sy.wait_ge(sem.sent, n["sent"])
 
-    ranks = sorted(range(N), key=lambda j: (dist(j), j))
-    near = [j for j in ranks if dist(j) < 2]
-    blocks = [(j, i) for j in near for i in range(WT)] + [(j, i) for i in range(WT) for j in ranks if j not in near]
+    ranks = sorted(range(N), key=lambda j: (hops(topo, topo.chip(core), topo.chip(cores[j])), j))
+    near = [j for j in ranks if topo.chip(cores[j]) == topo.chip(core)]
+    blocks = [(j, i) for w, i in ORDER for j in ranks if way[(core, j)] == w]
     te.wait_ge(sem.qd, 2)
     te.wait_ge(sem.xd, 1)
     for k, (j, i) in enumerate(blocks):
@@ -194,24 +233,25 @@ def rank_program(g, core, T, topo):
         if k >= 8:
             te.wait_ge(cp, (k - 8) // 2 + 1)
         if j != rank:
-            te.wait_ge(sem["a%dc%d" % (j, i)], got[(core, j)])
-            if i == 0:
-                te.wait_ge(sem["a%dp" % j], got[(core, j)])
+            for p in ("c%d" % i, "c", "p"):
+                if (core, j, p) in got and (i == 0 or p == "c1"):
+                    te.wait_ge(sem["a%d%s" % (j, p)], got[(core, j, p)])
         o = 512 * (k % 8)
         a = GW * j + NC * i
         te.matmul_mx(T.ps[:, o:o + NC], T.qc[:, a:a + NC], T.qs[:, a:a + NC], T.xq[:, :], T.xp[:, :],
                      True, True).then_inc(mm, 1)
         if k % 2:
             sc.wait_ge(mm, k // 2 + 1)
-            sc.activation(T.yb[:, a:a + NC], T.ps[:, o:o + NC], ActivationFunctionType.Copy).then_inc(cp, 1)
+            sc.activation(T.yb[:, a:a + NC], T.ps[:, o:o + NC], ActivationFunctionType.Copy, scale=1 / UP).then_inc(cp, 1)
         else:
             ve.wait_ge(mm, k // 2 + 1)
-            ve.tensor_copy(T.yb[:, a:a + NC], T.ps[:, o:o + NC]).then_inc(cp, 1)
+            ve.tensor_scalar(T.yb[:, a:a + NC], T.ps[:, o:o + NC], 1 / UP, None, AluOpType.mult).then_inc(cp, 1)
         sy.wait_ge(cp, k // 2 + 1)
         if j not in near:
             sy.dma_start(T.y[:, a:a + NC], T.yb[:, a:a + NC]).then_inc(sem.ys, 16)
         elif i == WT - 1:
             sy.dma_start(T.y[:, GW * j:GW * j + GW], T.yb[:, GW * j:GW * j + GW]).then_inc(sem.ys, 16)
 
-    g.wait_ge(sem.sent, n)
+    g.wait_ge(sem.sent, n["sent"])
+    g.wait_ge(sem.nsent, n["nsent"])
     sy.wait_ge(sem.ys, 16 * (len(near) + WT * (N - len(near))))

from concourse.bass import DstId, RemoteDMATransfer
from concourse.mybir import dt, AluOpType, ActivationFunctionType

N, WT, NC = 6, 2, 128
TC = 4 * NC
GW = WT * NC
SIM_CORES = 96
UP = 4.0

SCRATCH = {
    "z": ("sbuf", [128, TC + 4], "bfloat16"),
    "cmp": ("sbuf", [128, NC], "bfloat16"),
    "sq": ("sbuf", [128, 4 * NC], "float8_e4m3fn_x4"),
    "ss": ("sbuf", [128, 4 * NC], "uint8"),
    "wq": ("sbuf", [128, GW], "float8_e4m3fn_x4"),
    "wp": ("sbuf", [128, GW], "uint8"),
    "gb": ("sbuf", [128, WT * TC], "bfloat16"),
    "v": ("sbuf", [128, WT * TC], "bfloat16"),
    "xb": ("sbuf", [128, TC], "bfloat16"),
    "xq": ("sbuf", [128, NC], "float8_e4m3fn_x4"),
    "xp": ("sbuf", [128, NC], "uint8"),
    "qc": ("sbuf", [128, N * GW], "float8_e4m3fn_x4"),
    "qs": ("sbuf", [128, N * GW], "uint8"),
    "yb": ("sbuf", [128, N * GW], "float32"),
    "ps": ("psum", [128, 4096], "float32"),
}
FAR = ("c0", "p", "c1")
NEAR = ("c", "p")
TILES = {"c0": 1, "p": 2, "c1": 2, "c": 2}
ORDER = (("own", 0), ("own", 1), ("near", 0), ("near", 1), ("direct", 0), ("direct", 1), ("later", 0), ("later", 1),
         ("passed", 0), ("helper", 0), ("relay", 0), ("passed", 1), ("helper", 1), ("relay", 1))
SEMAPHORES = (["cd", "zd", "sqd", "lw0", "lw1", "lp", "lg0", "lg1", "lx", "md", "vd", "qd", "xd",
               "mv", "ms", "cv", "cs", "ys", "sent", "nsent"]
              + ["a%d%s" % (j, p) for j in range(N) for p in TILES])


def bits(m):
    return bin(m).count("1")


def hops(topo, a, b):
    return 0 if a == b else 1 if topo.same_plane(a, b) else 2 if topo.mates(a, b) else 3


def plan(cores, topo):
    chips = []
    for c in cores:
        if topo.chip(c) not in chips:
            chips.append(topo.chip(c))
    members = {k: [c for c in cores if topo.chip(c) == k] for k in chips}
    spare = {k: [c for c in range(SIM_CORES) if topo.chip(c) == k and c not in cores] for k in chips}
    load = {}
    on = {c: [] for c in cores}
    off = {c: [] for c in cores}
    ways = {}
    passed = {}
    way = {(c, cores.index(c)): "own" for c in cores}
    far = [(s, k) for s in cores for k in sorted(chips) if k != topo.chip(s)]
    direct = [(s, k) for s, k in far if topo.may_write(s, members[k][0])]
    for s, k in direct:
        w = (topo.chip(s), topo.die(s))
        load[w] = load.get(w, 0) + 1
    for s, k in far:
        if (s, k) in direct:
            continue
        own = [h for h in spare[topo.chip(s)] if topo.may_write(h, members[k][0])]
        h = min(own, key=lambda h: (load.get((topo.chip(h), topo.die(h)), 0), topo.die(h) != topo.die(s), h))
        spare[topo.chip(s)].remove(h)
        w = (topo.chip(h), topo.die(h))
        load[w] = load.get(w, 0) + len(members[k])
        on[s].append(h)
        ways[(h, s)] = {p: list(members[k]) for p in FAR}
        for d in members[k]:
            way[(d, cores.index(s))] = "helper"
    for s in cores:
        if not on[s]:
            continue
        own = [h for h in spare[topo.chip(s)] if all(topo.may_write(h, ways[(r, s)][FAR[0]][0]) for r in on[s])]
        x = min(own, key=lambda x: (sum(topo.die(x) == topo.die(r) for r in on[s]), x))
        spare[topo.chip(s)].remove(x)
        ways[(x, s)] = {FAR[0]: []}
        for r in on[s]:
            ways[(x, s)][FAR[0]] += ways[(r, s)][FAR[0]][1:]
            ways[(r, s)][FAR[0]] = ways[(r, s)][FAR[0]][:1]
        on[s].append(x)
    for s, k in sorted(direct, key=lambda w: hops(topo, topo.chip(w[0]), w[1])):
        j = cores.index(s)
        free = [h for h in members[k] if h not in [d for d, t in passed]]
        if free:
            h = free[0]
            passed[(h, s)] = [d for d in members[k] if d != h]
        else:
            h = min(spare[k], key=lambda h: (topo.die(h) != topo.die(members[k][0]), h))
            spare[k].remove(h)
            ways[(h, s)] = {p: list(members[k]) for p in FAR}
        off[s].append(h)
        for d in members[k]:
            way[(d, j)] = "direct" if d == h else "passed" if free else "relay"
    for s in cores:
        for d in members[topo.chip(s)]:
            if d != s:
                way[(d, cores.index(s))] = "later" if on[s] else "near"
    calls, got = {}, {}

    def add(c, s, p, tr, local):
        calls.setdefault(c, []).append((cores.index(s), p, tr, local))
        for m, ds in tr:
            for d in ds:
                got[(d, cores.index(s), p)] = bits(m)

    for s in cores:
        nb = [c for c in members[topo.chip(s)] if c != s]
        other = [c for c in cores if topo.chip(c) != topo.chip(s)]
        om = topo.mask(s, other[0])
        every = topo.mask(s, nb[0])
        rest = every & ~om
        for p in FAR:
            tr = []
            if off[s]:
                tr.append((om, off[s]))
            hs = [h for h in on[s] if p in ways[(h, s)]]
            if hs:
                tr.append((rest if off[s] else every, hs))
            add(s, s, p, tr, "sent")
        for p in NEAR:
            add(s, s, p, [(every if not off[s] else om if on[s] else rest, nb)], "nsent")
    for p in FAR:
        for (h, s), ds in passed.items():
            add(h, s, p, [(topo.mask(h, ds[0]), ds)], "nsent")
        for (h, s), w in ways.items():
            if p in w:
                add(h, s, p, [(topo.mask(h, w[p][0]), w[p])], "sent")
    return calls, got, way


def piece(T, j, p):
    a = GW * j
    if p == "p":
        return T.qs[:, a:a + GW]
    if p == "c":
        return T.qc[:, a:a + GW].bitcast(dt.uint8)
    i = int(p[1])
    return T.qc[:, a + NC * i:a + NC * (i + 1)].bitcast(dt.uint8)


def send(g, T, topo, j, p, tr, local):
    ap = piece(T, j, p)
    ts = []
    for m, ds in tr:
        ids = []
        for d in ds:
            a = topo.addr(d)
            ids.append(DstId(rid=a[0], pnc=a[1]))
        ts.append(RemoteDMATransfer(dst_ids=ids, dma_engine_mask=m, remote_sem=T.sem["a%d%s" % (j, p)],
                                    srcs=[ap], dsts=[ap] * len(ds)))
    g.remote_dma_fused(ts, local_sem=T.sem[local])
    return sum(bits(m) for m, ds in tr)


def rank_program(g, core, T, topo):
    cores = list(T.cores)
    calls, got, way = plan(cores, topo)
    rank = T.rank_of(core)
    if rank is None:
        n = 0
        for j, p, tr, local in calls.get(core, []):
            g.wait_ge(T.sem["a%d%s" % (j, p)], got[(core, j, p)])
            n += send(g, T, topo, j, p, tr, local)
        if n:
            g.wait_ge(T.sem.sent, n)
        return

    sem = T.sem
    me = GW * rank
    sy, sc, ve, te = g.sync, g.scalar, g.vector, g.tensor

    sc.dma_start(T.wp[:, :], T.ws[:, :]).then_inc(sem.lp, 16)
    for i in range(WT):
        sy.dma_start(T.wq[:, NC * i:NC * i + NC].bitcast(dt.uint8), T.wc[:, TC * i:TC * i + TC]).then_inc(sem["lw%d" % i], 16)
        sy.dma_start(T.gb[:, TC * i:TC * i + TC], T.gr[:, TC * i:TC * i + TC]).then_inc(sem["lg%d" % i], 16)
    sy.dma_start(T.xb[:, :], T.x[:, :]).then_inc(sem.lx, 16)

    g.iota(T.cmp[:, :], [[1, NC]], 0, -1, allow_small_or_imprecise_dtypes=True).then_inc(sem.cd, 1)
    ve.memset(T.z[:, :], 0.0).then_inc(sem.zd, 1)
    ve.wait_ge(sem.zd, 1)
    ve.wait_ge(sem.cd, 1)
    ve.tensor_scalar(T.z[:, 3:TC:4], T.cmp[:, :], 0.0, UP, AluOpType.is_equal, AluOpType.mult).then_inc(sem.zd, 1)
    ve.wait_ge(sem.zd, 2)
    for b in range(4):
        ve.quantize_mx(T.sq[:, NC * b:NC * b + NC], T.ss[:, NC * b:NC * b + NC],
                       T.z[:, 3 - b:3 - b + TC]).then_inc(sem.sqd, 1)

    te.wait_ge(sem.lp, 16)
    for i in range(WT):
        te.wait_ge(sem["lw%d" % i], 16)
        for b in range(4):
            if i == 0:
                te.wait_ge(sem.sqd, b + 1)
            o = 512 * (4 * i + b)
            te.matmul_mx(T.ps[:, o:o + NC], T.sq[:, NC * b:NC * b + NC], T.ss[:, NC * b:NC * b + NC],
                         T.wq[:, NC * i:NC * i + NC], T.wp[:, NC * i:NC * i + NC], True, True).then_inc(sem.md, 1)

    for i in range(WT):
        ve.wait_ge(sem["lg%d" % i], 16)
        for b in range(4):
            k = 4 * i + b
            ve.wait_ge(sem.md, k + 1)
            c0, c1 = TC * i + b, TC * (i + 1)
            ve.tensor_tensor(T.v[:, c0:c1:4], T.ps[:, 512 * k:512 * k + NC], T.gb[:, c0:c1:4],
                             AluOpType.subtract).then_inc(sem.vd, 1)
        ve.wait_ge(sem.vd, 4 * (i + 1))
        ve.quantize_mx(T.qc[:, me + NC * i:me + NC * i + NC], T.qs[:, me + NC * i:me + NC * i + NC],
                       T.v[:, TC * i:TC * (i + 1)]).then_inc(sem.qd, 1)
    ve.wait_ge(sem.lx, 16)
    ve.quantize_mx(T.xq[:, :], T.xp[:, :], T.xb[:, :]).then_inc(sem.xd, 1)

    n = {"sent": 0, "nsent": 0}
    for j, p, tr, local in calls[core]:
        if j == rank:
            g.wait_ge(sem.qd, TILES[p])
        else:
            g.wait_ge(sem["a%d%s" % (j, p)], got[(core, j, p)])
        n[local] += send(g, T, topo, j, p, tr, local)
    sy.wait_ge(sem.sent, n["sent"])

    ranks = sorted(range(N), key=lambda j: (hops(topo, topo.chip(core), topo.chip(cores[j])), j))
    near = [j for j in ranks if topo.chip(cores[j]) == topo.chip(core)]
    blocks = [(j, i) for w, i in ORDER for j in ranks if way[(core, j)] == w]
    te.wait_ge(sem.qd, 2)
    te.wait_ge(sem.xd, 1)
    for k, (j, i) in enumerate(blocks):
        mm, cp = (sem.ms, sem.cs) if k % 2 else (sem.mv, sem.cv)
        if k >= 8:
            te.wait_ge(cp, (k - 8) // 2 + 1)
        if j != rank:
            for p in ("c%d" % i, "c", "p"):
                if (core, j, p) in got and (i == 0 or p == "c1"):
                    te.wait_ge(sem["a%d%s" % (j, p)], got[(core, j, p)])
        o = 512 * (k % 8)
        a = GW * j + NC * i
        te.matmul_mx(T.ps[:, o:o + NC], T.qc[:, a:a + NC], T.qs[:, a:a + NC], T.xq[:, :], T.xp[:, :],
                     True, True).then_inc(mm, 1)
        if k % 2:
            sc.wait_ge(mm, k // 2 + 1)
            sc.activation(T.yb[:, a:a + NC], T.ps[:, o:o + NC], ActivationFunctionType.Copy, scale=1 / UP).then_inc(cp, 1)
        else:
            ve.wait_ge(mm, k // 2 + 1)
            ve.tensor_scalar(T.yb[:, a:a + NC], T.ps[:, o:o + NC], 1 / UP, None, AluOpType.mult).then_inc(cp, 1)
        sy.wait_ge(cp, k // 2 + 1)
        if j not in near:
            sy.dma_start(T.y[:, a:a + NC], T.yb[:, a:a + NC]).then_inc(sem.ys, 16)
        elif i == WT - 1:
            sy.dma_start(T.y[:, GW * j:GW * j + GW], T.yb[:, GW * j:GW * j + GW]).then_inc(sem.ys, 16)

    g.wait_ge(sem.sent, n["sent"])
    g.wait_ge(sem.nsent, n["nsent"])
    sy.wait_ge(sem.ys, 16 * (len(near) + WT * (N - len(near))))
